import numpy as np
import ml_dtypes


def mxq(x, axis, fmt="e4m3"):
    dtype, down = {"e4m3": (ml_dtypes.float8_e4m3fn, 7), "e5m2": (ml_dtypes.float8_e5m2, 14)}[fmt]
    v = np.moveaxis(np.asarray(x, np.float32).astype(ml_dtypes.bfloat16).astype(np.float64), axis, -1)
    blocks = v.reshape(v.shape[:-1] + (-1, 32))
    amax = np.abs(blocks).max(-1, keepdims=True)
    byte = np.maximum(np.where(amax > 0, np.frexp(amax)[1] - 1 + 127, 0) - down, 1)
    scale = np.exp2(byte - 127.0)
    codes = (blocks / scale).astype(np.float32).astype(dtype).astype(np.float64)
    return np.moveaxis((codes * scale).reshape(v.shape), -1, axis)


WIDE = False


def mx_kscale(k):
    if not WIDE:
        return np.ones(k)
    levels = np.array([30, -30])
    if k % 512:
        return np.exp2(np.random.permutation(np.resize(levels, k // 32))).repeat(32)
    a = np.empty((k // 512, 16))
    for p in range(k // 512):
        a[p, :8] = np.random.permutation(np.resize(levels, 8))
        for g in range(8):
            far = levels[np.abs(levels - a[p, g]) >= 10]
            a[p, g + 8] = far[np.random.randint(len(far))]
    return np.exp2(a.ravel()).repeat(32)


def f64(x):
    return np.asarray(x).astype(np.float64)


def striped(idx):
    return np.tile(np.asarray(idx).reshape(-1, 16).T, (8, 1)).astype(np.uint16)


def unstriped(offs):
    return offs[:16].T.reshape(-1).astype(np.int64)


E2M1 = np.array([0.0, 0.5, 1.0, 1.5, 2.0, 3.0, 4.0, 6.0, -0.0, -0.5, -1.0, -1.5, -2.0, -3.0, -4.0, -6.0])


def pack_weight(w, fmt):
    k, n = w.shape
    w = f64(np.asarray(w, np.float32).astype(ml_dtypes.bfloat16)).reshape(k // 32, 32, n)
    amax = np.abs(w).max(1)
    if fmt in ("e4m3", "e5m2"):
        byte = np.frexp(amax)[1] - 1 + 127 - (7 if fmt == "e4m3" else 14)
    else:
        mant, ex = np.frexp(amax / 6.0)
        byte = np.where(mant > 0.5, ex, ex - 1) + 127
    byte = np.clip(np.where(amax > 0, byte, 1), 1, 254)
    scaled = (w * np.exp2(127.0 - byte)[:, None, :]).reshape(k, n).astype(np.float32)
    by_word = np.ascontiguousarray(scaled.reshape(k // 512, 128, 4, n).transpose(0, 1, 3, 2))
    if fmt in ("e4m3", "e5m2"):
        words = by_word.astype(ml_dtypes.float8_e4m3fn if fmt == "e4m3" else ml_dtypes.float8_e5m2).view(np.uint8)
    else:
        c = by_word.astype(ml_dtypes.float4_e2m1fn).view(np.uint8) & 0xF
        words = (c[..., 0::2] | (c[..., 1::2] << 4)).reshape(k // 512, 128, 2 * n)
    return np.ascontiguousarray(words), np.ascontiguousarray(byte.astype(np.uint8).reshape(k // 512, 16, n))


def unpack_weight(words, scales, fmt):
    g, _, n = scales.shape
    words = np.ascontiguousarray(words).reshape(g, 128, n, -1)
    if fmt in ("e4m3", "e5m2"):
        vals = words.view(ml_dtypes.float8_e4m3fn if fmt == "e4m3" else ml_dtypes.float8_e5m2).astype(np.float64)
    else:
        nib = np.empty((g, 128, n, 4), np.uint8)
        nib[..., 0::2] = words & 0xF
        nib[..., 1::2] = words >> 4
        vals = E2M1[nib]
    vals = vals * np.repeat(np.exp2(scales.astype(np.float64) - 127.0), 8, axis=1)[..., None]
    return vals.transpose(0, 1, 3, 2).reshape(g * 512, n)


K, T, Z, J, R, C, O, N, E = 512, 1024, 1024, 256, 512, 512, 256, 256, 1024


def setup_inputs():
    n = np.random.standard_normal
    idx = np.random.permutation(T)[:J]
    idx2 = np.random.permutation(Z)[:J]
    idx3 = np.random.permutation(C)[:J]
    idx4 = np.random.permutation(C)[:J]
    idx5 = np.random.permutation(C)[:O]
    idx6 = np.random.permutation(C)[:O]
    idx7 = np.random.permutation(E)[:O]
    fk = mx_kscale(K)
    fr = mx_kscale(R)
    xtp = pack_weight(n((K, T)) / fk[:, None], "e2m1")
    xop = pack_weight(n((K, Z)) / fk[:, None], "e4m3")
    wp = pack_weight(n((K, R)) * 1 / np.sqrt(K) * fk[:, None] * fr, "e4m3")
    w2p = pack_weight(n((K, R)) * 1 / np.sqrt(K) * fk[:, None] * fr, "e5m2")
    wbp = pack_weight(n((R, N)) * 1 / np.sqrt(R) / fr[:, None], "e2m1")
    return {
        "xt_words": xtp[0],
        "xt_scales": xtp[1],
        "xo_words": xop[0],
        "xo_scales": xop[1],
        "w_words": wp[0],
        "w_scales": wp[1],
        "w2_words": w2p[0],
        "w2_scales": w2p[1],
        "wb_words": wbp[0],
        "wb_scales": wbp[1],
        "tz": (n((N, E))).astype(np.float32),
        "offs": striped(idx),
        "offs2": striped(idx2),
        "offs3": striped(idx3),
        "offs4": striped(idx4),
        "offs5": striped(idx5),
        "offs6": striped(idx6),
        "offs7": striped(idx7),
    }


def reference(xt_words, xt_scales, xo_words, xo_scales, w_words, w_scales, w2_words, w2_scales, wb_words, wb_scales, tz, offs, offs2, offs3, offs4, offs5, offs6, offs7):
    idx = unstriped(offs)
    idx2 = unstriped(offs2)
    idx3 = unstriped(offs3)
    idx4 = unstriped(offs4)
    idx5 = unstriped(offs5)
    idx6 = unstriped(offs6)
    idx7 = unstriped(offs7)
    xtu = unpack_weight(xt_words, xt_scales, "e2m1")
    xou = unpack_weight(xo_words, xo_scales, "e4m3")
    wu = unpack_weight(w_words, w_scales, "e4m3")
    w2u = unpack_weight(w2_words, w2_scales, "e5m2")
    wbu = unpack_weight(wb_words, wb_scales, "e2m1")
    xtidxg = xtu[:, idx]
    xoidx2g = xou[:, idx2]
    a = wu.T @ xtidxg + w2u.T @ xoidx2g
    b = w2u.T @ xtidxg + wu.T @ xoidx2g
    pw = np.zeros((R, C))
    pw[:, idx3] = a
    pv = np.zeros((R, C))
    pv[:, idx4] = b
    hid = np.abs(pw[:, idx5] - pv[:, idx6])
    hidq = mxq(hid, 0, "e5m2")
    p = wbu.T @ hidq
    y = p + f64(tz)[:, idx7]
    return y

@@ -1,0 +1,202 @@
+from contextlib import ExitStack
+
+import concourse.mybir as mybir
+
+K, T, Z, J, R, C, O, N, E = 512, 1024, 1024, 256, 512, 512, 256, 256, 1024
+FLOPS = 2 * (4 * K * R * J + R * N * O)
+
+F32 = mybir.dt.float32
+BF16 = mybir.dt.bfloat16
+I32 = mybir.dt.int32
+U32 = mybir.dt.uint32
+U16 = mybir.dt.uint16
+U8 = mybir.dt.uint8
+E4M3 = mybir.dt.float8_e4m3fn_x4
+E5M2 = mybir.dt.float8_e5m2_x4
+E2M1 = mybir.dt.float4_e2m1fn_x4
+ACT = mybir.ActivationFunctionType
+ALU = mybir.AluOpType
+
+P = 128
+PACK = 4
+
+
+def tile_list_crossed_twoboards_one_tabled_kernel(
+    tc, xt_words, xt_scales, xo_words, xo_scales, w_words, w_scales, w2_words, w2_scales,
+    wb_words, wb_scales, tz, offs, offs2, offs3, offs4, offs5, offs6, offs7, out,
+):
+    nc = tc.nc
+    with ExitStack() as ctx:
+        lists = ctx.enter_context(tc.tile_pool(name="lists", bufs=1))
+        sb = ctx.enter_context(tc.tile_pool(name="sb", bufs=1))
+        psum = ctx.enter_context(tc.psum_pool(name="psum", bufs=1))
+
+        def load_list(src, name):
+            tile = lists.tile([P, J // 16], U16, name=name)
+            nc.sync.dma_start(tile[:], src)
+            return tile
+
+        def plane_tile(width, name):
+            return sb.tile([P, width], U8, name=name, align_bytes=64)
+
+        def load_quadrant(plane, scales, q):
+            rows = scales[0, 4 * q : 4 * q + 4, :].bitcast(I32)
+            nc.sync.dma_start(plane[32 * q : 32 * q + 32, :].bitcast(I32), rows.partition_broadcast(8))
+
+        def load_words(words, width, name, tag):
+            tile = sb.tile([P, width], U32, name=name, tag=tag, align_bytes=64)
+            nc.sync.dma_start(tile[:].bitcast(I32), words[0].rearrange("p c t -> p (c t)").bitcast(I32))
+            return tile
+
+        xt_s = plane_tile(T, "xt_s")
+        xo_s = plane_tile(Z, "xo_s")
+        w_s = plane_tile(R, "w_s")
+        w2_s = plane_tile(R, "w2_s")
+        wb_s = plane_tile(N, "wb_s")
+
+        idx = load_list(offs, "idx")
+        for q in range(4):
+            load_quadrant(xt_s, xt_scales, q)
+        idx2 = load_list(offs2, "idx2")
+        xt_w = sb.tile([P, T], U16, name="xt_w", tag="early0", align_bytes=64)
+        nc.sync.dma_start(xt_w[:].bitcast(I32), xt_words[0].bitcast(I32))
+        xo_w = load_words(xo_words, Z, "xo_w", "early1")
+        for q in range(4):
+            load_quadrant(w_s, w_scales, q)
+        for q in range(2):
+            load_quadrant(xo_s, xo_scales, q)
+        w_w = load_words(w_words, R, "w_w", "w_w")
+        w2_w = load_words(w2_words, R, "w2_w", "w2_w")
+        for q in range(2, 4):
+            load_quadrant(xo_s, xo_scales, q)
+        for q in range(4):
+            load_quadrant(w2_s, w2_scales, q)
+        idx3 = load_list(offs3, "idx3")
+        idx4 = load_list(offs4, "idx4")
+        idx5 = load_list(offs5, "idx5")
+        idx6 = load_list(offs6, "idx6")
+        wb_w = sb.tile([P, 2 * N], U8, name="wb_w", align_bytes=64)
+        nc.sync.dma_start(wb_w[:].bitcast(I32), wb_words[0].bitcast(I32))
+        for q in range(4):
+            load_quadrant(wb_s, wb_scales, q)
+        idx7 = load_list(offs7, "idx7")
+
+        pw = [sb.tile([P, C], F32, name="pw%d" % t) for t in range(PACK)]
+        pv = [sb.tile([P, C], F32, name="pv%d" % t) for t in range(PACK)]
+        for t in range(PACK):
+            clear = nc.vector.memset if t < 2 else nc.gpsimd.memset
+            clear(pw[t][:], 0.0)
+            clear(pv[t][:], 0.0)
+
+        xt_gs = sb.tile([P, J], U8, name="xt_gs", align_bytes=64)
+        nc.vector.tensor_copy(xt_gs[:], xt_s[:].indirect(idx[:]))
+        xt_gw = sb.tile([P, J], U16, name="xt_gw", align_bytes=64)
+        nc.vector.tensor_copy(xt_gw[:], xt_w[:].indirect(idx[:]))
+        xo_gw = sb.tile([P, J], U32, name="xo_gw", align_bytes=64)
+        nc.vector.tensor_copy(xo_gw[:], xo_w[:].indirect(idx2[:]))
+
+        def dealt(src, dtype, run, name, copy):
+            dst = sb.tile([P, R], dtype, name=name, align_bytes=64)
+            copy(
+                dst[:].rearrange("p (t c i) -> p c t i", t=PACK, i=run),
+                src[:].rearrange("p (c i t) -> p c t i", t=PACK, i=run),
+            )
+            return dst
+
+        w_dw = dealt(w_w, U32, 4, "w_dw", nc.scalar.copy)
+        w2_dw = dealt(w2_w, U32, 4, "w2_dw", nc.scalar.copy)
+        w_ds = dealt(w_s, U8, 16, "w_ds", nc.vector.tensor_copy)
+        xo_gs = sb.tile([P, J], U8, name="xo_gs", align_bytes=64)
+        nc.vector.tensor_copy(xo_gs[:], xo_s[:].indirect(idx2[:]))
+        w2_ds = dealt(w2_s, U8, 16, "w2_ds", nc.vector.tensor_copy)
+
+        tz_rows = []
+        for h in range(N // P):
+            rows = sb.tile([P, E], F32, name="tz%d" % h, tag="early%d" % h, align_bytes=64)
+            nc.sync.dma_start(rows[:], tz[h * P : (h + 1) * P, :])
+            tz_rows.append(rows)
+
+        def mx_pass(acc, t, weight, picked, first):
+            cols = slice(t * P, (t + 1) * P)
+            words, scales, fmt = weight
+            g_words, g_scales, g_fmt = picked
+            nc.tensor.matmul_mx(
+                out=acc[:], lhsT=words[:, cols].bitcast(fmt), lhsT_scale=scales[:, cols],
+                rhs=g_words[:].bitcast(g_fmt), rhs_scale=g_scales[:],
+                start=first, stop=not first,
+            )
+
+        first_w = (w_dw, w_ds, E4M3)
+        second_w = (w2_dw, w2_ds, E5M2)
+        tokens = (xt_gw, xt_gs, E2M1)
+        notes = (xo_gw, xo_gs, E4M3)
+        a_ps = [psum.tile([P, J], F32, name="a_ps%d" % t, tag="a%d" % t) for t in range(PACK)]
+        b_ps = [psum.tile([P, J], F32, name="b_ps%d" % t, tag="b%d" % t) for t in range(PACK)]
+        for t in range(PACK):
+            mx_pass(a_ps[t], t, first_w, tokens, True)
+        stage = sb.tile([P, PACK, O], F32, name="stage")
+        b_first = sb.tile([P, J], F32, name="b_first")
+        pw_g = []
+
+        def difference(t):
+            nc.vector.tensor_tensor(stage[:, t, :], pv[t][:].indirect(idx6[:]), pw_g[t][:], ALU.subtract)
+
+        for t in range(PACK):
+            mx_pass(b_ps[t], t, first_w, notes, True)
+            mx_pass(b_ps[t], t, second_w, tokens, False)
+            mx_pass(a_ps[t], t, second_w, notes, False)
+            a_sb = sb.tile([P, J], F32, name="a_sb%d" % t, tag="a_sb%d" % t, align_bytes=64)
+            nc.scalar.activation(a_sb[:], a_ps[t][:], ACT.Copy)
+            b_sb = b_first[:] if t == 0 else stage[:, t - 1, :]
+            nc.vector.tensor_copy(b_sb, b_ps[t][:])
+            if t >= 1:
+                picked = sb.tile([P, O], F32, name="pw_g%d" % (t - 1))
+                nc.scalar.activation(picked[:], pw[t - 1][:].indirect(idx5[:]), ACT.Copy)
+                pw_g.append(picked)
+            if t >= 2:
+                difference(t - 2)
+            nc.scalar.activation(pw[t][:].indirect(idx3[:]), a_sb[:], ACT.Copy)
+            nc.vector.tensor_copy(pv[t][:].indirect(idx4[:]), b_sb)
+        picked = sb.tile([P, O], F32, name="pw_g3")
+        nc.scalar.activation(picked[:], pw[3][:].indirect(idx5[:]), ACT.Copy)
+        pw_g.append(picked)
+        difference(2)
+        difference(3)
+
+        hid = sb.tile([P, O, PACK], BF16, name="hid", tag="a_sb3", align_bytes=64)
+
+        def magnitude(pair, o_cols):
+            nc.scalar.activation(
+                hid[:, o_cols, pair].rearrange("p (c i) t -> p c t i", i=4),
+                stage[:, pair, o_cols].rearrange("p t (c i) -> p c t i", i=4),
+                ACT.Abs,
+            )
+
+        magnitude(slice(0, 2), slice(0, O))
+
+        half = O // 2
+        halves = [slice(u * half, (u + 1) * half) for u in range(2)]
+        idx7_halves = [idx7[:, u * (half // 16) : (u + 1) * (half // 16)] for u in range(2)]
+        hid_w = sb.tile([P, O], U32, name="hid_w", align_bytes=64)
+        hid_s = sb.tile([P, O], U8, name="hid_s", align_bytes=64)
+        for u in range(2):
+            magnitude(slice(2, 4), halves[u])
+            nc.vector.tensor_copy(stage[:, u, halves[0]], tz_rows[u][:].indirect(idx7_halves[0]))
+            nc.vector.quantize_mx(
+                out=hid_w[:, halves[u]].bitcast(E5M2), scales=hid_s[:, halves[u]],
+                in_=hid[:, halves[u], :].rearrange("p o t -> p (o t)"),
+            )
+        for h in range(N // P):
+            nc.scalar.activation(stage[:, h, halves[1]], tz_rows[h][:].indirect(idx7_halves[1]), ACT.Copy)
+        for u in range(2):
+            o_cols = slice(u * half, (u + 1) * half)
+            p_ps = psum.tile([P, N // P, half], F32, name="p_ps%d" % u, tag="a%d" % u)
+            for h in range(N // P):
+                nc.tensor.matmul_mx(
+                    out=p_ps[:, h, :], lhsT=wb_w[:, 2 * h * P : 2 * (h + 1) * P].bitcast(E2M1),
+                    lhsT_scale=wb_s[:, h * P : (h + 1) * P],
+                    rhs=hid_w[:, o_cols].bitcast(E5M2), rhs_scale=hid_s[:, o_cols], start=True, stop=True,
+                )
+            y = sb.tile([P, N // P, half], F32, name="y%d" % u)
+            nc.vector.tensor_tensor(y[:], p_ps[:], stage[:, 0:2, o_cols], ALU.add)
+            nc.sync.dma_start(out[:, o_cols].rearrange("(h p) o -> p h o", p=P), y[:])

@@ -95,20 +95,26 @@ def tile_list_crossed_twoboards_one_tabled_kernel(
         xo_gw = sb.tile([P, J], U32, name="xo_gw", align_bytes=64)
         nc.vector.tensor_copy(xo_gw[:], xo_w[:].indirect(idx2[:]))
 
-        def dealt(src, dtype, run, name, copy):
-            dst = sb.tile([P, R], dtype, name=name, align_bytes=64)
-            copy(
-                dst[:].rearrange("p (t c i) -> p c t i", t=PACK, i=run),
-                src[:].rearrange("p (c i t) -> p c t i", t=PACK, i=run),
-            )
-            return dst
+        def dealt(src, dtype, run, name, copy, groups):
+            slices = []
+            for first, last in groups:
+                dst = sb.tile([P, (last - first) * P], dtype, name="%s%d" % (name, first), align_bytes=64)
+                copy(
+                    dst[:].rearrange("p (t c i) -> p c t i", t=last - first, i=run),
+                    src[:].rearrange("p (c i t) -> p c t i", t=PACK, i=run)[:, :, first:last, :],
+                )
+                slices.extend(dst[:, n * P : (n + 1) * P] for n in range(last - first))
+            return slices
 
-        w_dw = dealt(w_w, U32, 4, "w_dw", nc.scalar.copy)
-        w2_dw = dealt(w2_w, U32, 4, "w2_dw", nc.scalar.copy)
-        w_ds = dealt(w_s, U8, 16, "w_ds", nc.vector.tensor_copy)
+        whole = [(0, PACK)]
+        first_apart = [(0, 1), (1, PACK)]
+
+        w_dw = dealt(w_w, U32, 4, "w_dw", nc.scalar.copy, whole)
+        w2_dw = dealt(w2_w, U32, 4, "w2_dw", nc.scalar.copy, first_apart)
+        w_ds = dealt(w_s, U8, 16, "w_ds", nc.vector.tensor_copy, whole)
         xo_gs = sb.tile([P, J], U8, name="xo_gs", align_bytes=64)
         nc.vector.tensor_copy(xo_gs[:], xo_s[:].indirect(idx2[:]))
-        w2_ds = dealt(w2_s, U8, 16, "w2_ds", nc.vector.tensor_copy)
+        w2_ds = dealt(w2_s, U8, 16, "w2_ds", nc.vector.tensor_copy, first_apart)
 
         tz_rows = []
         for h in range(N // P):
@@ -117,11 +123,10 @@ def tile_list_crossed_twoboards_one_tabled_kernel(
             tz_rows.append(rows)
 
         def mx_pass(acc, t, weight, picked, first):
-            cols = slice(t * P, (t + 1) * P)
             words, scales, fmt = weight
             g_words, g_scales, g_fmt = picked
             nc.tensor.matmul_mx(
-                out=acc[:], lhsT=words[:, cols].bitcast(fmt), lhsT_scale=scales[:, cols],
+                out=acc[:], lhsT=words[t].bitcast(fmt), lhsT_scale=scales[t],
                 rhs=g_words[:].bitcast(g_fmt), rhs_scale=g_scales[:],
                 start=first, stop=not first,
             )
@@ -146,48 +151,52 @@ def tile_list_crossed_twoboards_one_tabled_kernel(
             mx_pass(b_ps[t], t, second_w, tokens, False)
             mx_pass(a_ps[t], t, second_w, notes, False)
             a_sb = sb.tile([P, J], F32, name="a_sb%d" % t, tag="a_sb%d" % t, align_bytes=64)
-            nc.scalar.activation(a_sb[:], a_ps[t][:], ACT.Copy)
+            if t < PACK - 1:
+                nc.scalar.activation(a_sb[:], a_ps[t][:], ACT.Copy)
+            else:
+                nc.vector.tensor_copy(a_sb[:], a_ps[t][:])
             b_sb = b_first[:] if t == 0 else stage[:, t - 1, :]
             nc.vector.tensor_copy(b_sb, b_ps[t][:])
             if t >= 1:
-                picked = sb.tile([P, O], F32, name="pw_g%d" % (t - 1))
+                picked = sb.tile([P, O], F32, name="pw_g%d" % (t - 1), tag="pw_g%d" % (t - 1))
                 nc.scalar.activation(picked[:], pw[t - 1][:].indirect(idx5[:]), ACT.Copy)
                 pw_g.append(picked)
             if t >= 2:
                 difference(t - 2)
             nc.scalar.activation(pw[t][:].indirect(idx3[:]), a_sb[:], ACT.Copy)
             nc.vector.tensor_copy(pv[t][:].indirect(idx4[:]), b_sb)
-        picked = sb.tile([P, O], F32, name="pw_g3")
+        picked = sb.tile([P, O], F32, name="pw_g3", tag="pw_g3")
         nc.scalar.activation(picked[:], pw[3][:].indirect(idx5[:]), ACT.Copy)
         pw_g.append(picked)
         difference(2)
         difference(3)
 
-        hid = sb.tile([P, O, PACK], BF16, name="hid", tag="a_sb3", align_bytes=64)
-
-        def magnitude(pair, o_cols):
-            nc.scalar.activation(
-                hid[:, o_cols, pair].rearrange("p (c i) t -> p c t i", i=4),
-                stage[:, pair, o_cols].rearrange("p t (c i) -> p c t i", i=4),
-                ACT.Abs,
-            )
-
-        magnitude(slice(0, 2), slice(0, O))
-
         half = O // 2
         halves = [slice(u * half, (u + 1) * half) for u in range(2)]
         idx7_halves = [idx7[:, u * (half // 16) : (u + 1) * (half // 16)] for u in range(2)]
-        hid_w = sb.tile([P, O], U32, name="hid_w", align_bytes=64)
-        hid_s = sb.tile([P, O], U8, name="hid_s", align_bytes=64)
-        for u in range(2):
-            magnitude(slice(2, 4), halves[u])
-            nc.vector.tensor_copy(stage[:, u, halves[0]], tz_rows[u][:].indirect(idx7_halves[0]))
-            nc.vector.quantize_mx(
-                out=hid_w[:, halves[u]].bitcast(E5M2), scales=hid_s[:, halves[u]],
-                in_=hid[:, halves[u], :].rearrange("p o t -> p (o t)"),
+        hid = [
+            sb.tile([P, half * PACK], BF16, name="hid%d" % u, tag=tag, align_bytes=64)
+            for u, tag in enumerate(("a_sb3", "hid1"))
+        ]
+
+        def magnitude(u, pair):
+            nc.scalar.activation(
+                hid[u][:].rearrange("p (c i t) -> p c t i", i=4, t=PACK)[:, :, pair, :],
+                stage[:, pair, halves[u]].rearrange("p t (c i) -> p c t i", i=4),
+                ACT.Abs,
             )
-        for h in range(N // P):
-            nc.scalar.activation(stage[:, h, halves[1]], tz_rows[h][:].indirect(idx7_halves[1]), ACT.Copy)
+
+        for u in range(2):
+            magnitude(u, slice(0, 2))
+        hid_w = [sb.tile([P, half], U32, name="hid_w%d" % u, align_bytes=64) for u in range(2)]
+        hid_s = [sb.tile([P, half], U8, name="hid_s%d" % u, align_bytes=64) for u in range(2)]
+        tz_g = sb.tile([P, 2, N // P, half], F32, name="tz_g", tag="pw_g3")
+        nc.vector.tensor_copy(tz_g[:, 0, 0, :], tz_rows[0][:].indirect(idx7_halves[0]))
+        for u in range(2):
+            magnitude(u, slice(2, 4))
+            nc.vector.quantize_mx(out=hid_w[u][:].bitcast(E5M2), scales=hid_s[u][:], in_=hid[u][:])
+        for u, h in ((0, 1), (1, 0), (1, 1)):
+            nc.scalar.activation(tz_g[:, u, h, :], tz_rows[h][:].indirect(idx7_halves[u]), ACT.Copy)
         for u in range(2):
             o_cols = slice(u * half, (u + 1) * half)
             p_ps = psum.tile([P, N // P, half], F32, name="p_ps%d" % u, tag="a%d" % u)
@@ -195,8 +204,8 @@ def tile_list_crossed_twoboards_one_tabled_kernel(
                 nc.tensor.matmul_mx(
                     out=p_ps[:, h, :], lhsT=wb_w[:, 2 * h * P : 2 * (h + 1) * P].bitcast(E2M1),
                     lhsT_scale=wb_s[:, h * P : (h + 1) * P],
-                    rhs=hid_w[:, o_cols].bitcast(E5M2), rhs_scale=hid_s[:, o_cols], start=True, stop=True,
+                    rhs=hid_w[u][:].bitcast(E5M2), rhs_scale=hid_s[u][:], start=True, stop=True,
                 )
             y = sb.tile([P, N // P, half], F32, name="y%d" % u)
-            nc.vector.tensor_tensor(y[:], p_ps[:], stage[:, 0:2, o_cols], ALU.add)
+            nc.vector.tensor_tensor(y[:], p_ps[:], tz_g[:, u, :, :], ALU.add)
             nc.sync.dma_start(out[:, o_cols].rearrange("(h p) o -> p h o", p=P), y[:])

from contextlib import ExitStack

import concourse.mybir as mybir

K, T, Z, J, R, C, O, N, E = 512, 1024, 1024, 256, 512, 512, 256, 256, 1024
FLOPS = 2 * (4 * K * R * J + R * N * O)

F32 = mybir.dt.float32
BF16 = mybir.dt.bfloat16
I32 = mybir.dt.int32
U32 = mybir.dt.uint32
U16 = mybir.dt.uint16
U8 = mybir.dt.uint8
E4M3 = mybir.dt.float8_e4m3fn_x4
E5M2 = mybir.dt.float8_e5m2_x4
E2M1 = mybir.dt.float4_e2m1fn_x4
ACT = mybir.ActivationFunctionType
ALU = mybir.AluOpType

P = 128
PACK = 4


def tile_list_crossed_twoboards_one_tabled_kernel(
    tc, xt_words, xt_scales, xo_words, xo_scales, w_words, w_scales, w2_words, w2_scales,
    wb_words, wb_scales, tz, offs, offs2, offs3, offs4, offs5, offs6, offs7, out,
):
    nc = tc.nc
    with ExitStack() as ctx:
        lists = ctx.enter_context(tc.tile_pool(name="lists", bufs=1))
        sb = ctx.enter_context(tc.tile_pool(name="sb", bufs=1))
        psum = ctx.enter_context(tc.psum_pool(name="psum", bufs=1))

        def load_list(src, name):
            tile = lists.tile([P, J // 16], U16, name=name)
            nc.sync.dma_start(tile[:], src)
            return tile

        def plane_tile(width, name):
            return sb.tile([P, width], U8, name=name, align_bytes=64)

        def load_quadrant(plane, scales, q):
            rows = scales[0, 4 * q : 4 * q + 4, :].bitcast(I32)
            nc.sync.dma_start(plane[32 * q : 32 * q + 32, :].bitcast(I32), rows.partition_broadcast(8))

        def load_words(words, width, name, tag):
            tile = sb.tile([P, width], U32, name=name, tag=tag, align_bytes=64)
            nc.sync.dma_start(tile[:].bitcast(I32), words[0].rearrange("p c t -> p (c t)").bitcast(I32))
            return tile

        xt_s = plane_tile(T, "xt_s")
        xo_s = plane_tile(Z, "xo_s")
        w_s = plane_tile(R, "w_s")
        w2_s = plane_tile(R, "w2_s")
        wb_s = plane_tile(N, "wb_s")

        idx = load_list(offs, "idx")
        for q in range(4):
            load_quadrant(xt_s, xt_scales, q)
        idx2 = load_list(offs2, "idx2")
        xt_w = sb.tile([P, T], U16, name="xt_w", tag="early0", align_bytes=64)
        nc.sync.dma_start(xt_w[:].bitcast(I32), xt_words[0].bitcast(I32))
        xo_w = load_words(xo_words, Z, "xo_w", "early1")
        for q in range(4):
            load_quadrant(w_s, w_scales, q)
        for q in range(2):
            load_quadrant(xo_s, xo_scales, q)
        w_w = load_words(w_words, R, "w_w", "w_w")
        w2_w = load_words(w2_words, R, "w2_w", "w2_w")
        for q in range(2, 4):
            load_quadrant(xo_s, xo_scales, q)
        for q in range(4):
            load_quadrant(w2_s, w2_scales, q)
        idx3 = load_list(offs3, "idx3")
        idx4 = load_list(offs4, "idx4")
        idx5 = load_list(offs5, "idx5")
        idx6 = load_list(offs6, "idx6")
        wb_w = sb.tile([P, 2 * N], U8, name="wb_w", align_bytes=64)
        nc.sync.dma_start(wb_w[:].bitcast(I32), wb_words[0].bitcast(I32))
        for q in range(4):
            load_quadrant(wb_s, wb_scales, q)
        idx7 = load_list(offs7, "idx7")

        pw = [sb.tile([P, C], F32, name="pw%d" % t) for t in range(PACK)]
        pv = [sb.tile([P, C], F32, name="pv%d" % t) for t in range(PACK)]
        for t in range(PACK):
            clear = nc.vector.memset if t < 2 else nc.gpsimd.memset
            clear(pw[t][:], 0.0)
            clear(pv[t][:], 0.0)

        xt_gs = sb.tile([P, J], U8, name="xt_gs", align_bytes=64)
        nc.vector.tensor_copy(xt_gs[:], xt_s[:].indirect(idx[:]))
        xt_gw = sb.tile([P, J], U16, name="xt_gw", align_bytes=64)
        nc.vector.tensor_copy(xt_gw[:], xt_w[:].indirect(idx[:]))
        xo_gw = sb.tile([P, J], U32, name="xo_gw", align_bytes=64)
        nc.vector.tensor_copy(xo_gw[:], xo_w[:].indirect(idx2[:]))

        def dealt(src, dtype, run, name, copy, groups):
            slices = []
            for first, last in groups:
                dst = sb.tile([P, (last - first) * P], dtype, name="%s%d" % (name, first), align_bytes=64)
                copy(
                    dst[:].rearrange("p (t c i) -> p c t i", t=last - first, i=run),
                    src[:].rearrange("p (c i t) -> p c t i", t=PACK, i=run)[:, :, first:last, :],
                )
                slices.extend(dst[:, n * P : (n + 1) * P] for n in range(last - first))
            return slices

        whole = [(0, PACK)]
        first_apart = [(0, 1), (1, PACK)]

        w_dw = dealt(w_w, U32, 4, "w_dw", nc.scalar.copy, whole)
        w2_dw = dealt(w2_w, U32, 4, "w2_dw", nc.scalar.copy, first_apart)
        w_ds = dealt(w_s, U8, 16, "w_ds", nc.vector.tensor_copy, whole)
        xo_gs = sb.tile([P, J], U8, name="xo_gs", align_bytes=64)
        nc.vector.tensor_copy(xo_gs[:], xo_s[:].indirect(idx2[:]))
        w2_ds = dealt(w2_s, U8, 16, "w2_ds", nc.vector.tensor_copy, first_apart)

        tz_rows = []
        for h in range(N // P):
            rows = sb.tile([P, E], F32, name="tz%d" % h, tag="early%d" % h, align_bytes=64)
            nc.sync.dma_start(rows[:], tz[h * P : (h + 1) * P, :])
            tz_rows.append(rows)

        def mx_pass(acc, t, weight, picked, first):
            words, scales, fmt = weight
            g_words, g_scales, g_fmt = picked
            nc.tensor.matmul_mx(
                out=acc[:], lhsT=words[t].bitcast(fmt), lhsT_scale=scales[t],
                rhs=g_words[:].bitcast(g_fmt), rhs_scale=g_scales[:],
                start=first, stop=not first,
            )

        first_w = (w_dw, w_ds, E4M3)
        second_w = (w2_dw, w2_ds, E5M2)
        tokens = (xt_gw, xt_gs, E2M1)
        notes = (xo_gw, xo_gs, E4M3)
        a_ps = [psum.tile([P, J], F32, name="a_ps%d" % t, tag="a%d" % t) for t in range(PACK)]
        b_ps = [psum.tile([P, J], F32, name="b_ps%d" % t, tag="b%d" % t) for t in range(PACK)]
        for t in range(PACK):
            mx_pass(a_ps[t], t, first_w, tokens, True)
        stage = sb.tile([P, PACK, O], F32, name="stage")
        b_first = sb.tile([P, J], F32, name="b_first")
        pw_g = []

        def difference(t):
            nc.vector.tensor_tensor(stage[:, t, :], pv[t][:].indirect(idx6[:]), pw_g[t][:], ALU.subtract)

        for t in range(PACK):
            mx_pass(b_ps[t], t, first_w, notes, True)
            mx_pass(b_ps[t], t, second_w, tokens, False)
            mx_pass(a_ps[t], t, second_w, notes, False)
            a_sb = sb.tile([P, J], F32, name="a_sb%d" % t, tag="a_sb%d" % t, align_bytes=64)
            if t < PACK - 1:
                nc.scalar.activation(a_sb[:], a_ps[t][:], ACT.Copy)
            else:
                nc.vector.tensor_copy(a_sb[:], a_ps[t][:])
            b_sb = b_first[:] if t == 0 else stage[:, t - 1, :]
            nc.vector.tensor_copy(b_sb, b_ps[t][:])
            if t >= 1:
                picked = sb.tile([P, O], F32, name="pw_g%d" % (t - 1), tag="pw_g%d" % (t - 1))
                nc.scalar.activation(picked[:], pw[t - 1][:].indirect(idx5[:]), ACT.Copy)
                pw_g.append(picked)
            if t >= 2:
                difference(t - 2)
            nc.scalar.activation(pw[t][:].indirect(idx3[:]), a_sb[:], ACT.Copy)
            nc.vector.tensor_copy(pv[t][:].indirect(idx4[:]), b_sb)
        picked = sb.tile([P, O], F32, name="pw_g3", tag="pw_g3")
        nc.scalar.activation(picked[:], pw[3][:].indirect(idx5[:]), ACT.Copy)
        pw_g.append(picked)
        difference(2)
        difference(3)

        half = O // 2
        halves = [slice(u * half, (u + 1) * half) for u in range(2)]
        idx7_halves = [idx7[:, u * (half // 16) : (u + 1) * (half // 16)] for u in range(2)]
        hid = [
            sb.tile([P, half * PACK], BF16, name="hid%d" % u, tag=tag, align_bytes=64)
            for u, tag in enumerate(("a_sb3", "hid1"))
        ]

        def magnitude(u, pair):
            nc.scalar.activation(
                hid[u][:].rearrange("p (c i t) -> p c t i", i=4, t=PACK)[:, :, pair, :],
                stage[:, pair, halves[u]].rearrange("p t (c i) -> p c t i", i=4),
                ACT.Abs,
            )

        for u in range(2):
            magnitude(u, slice(0, 2))
        hid_w = [sb.tile([P, half], U32, name="hid_w%d" % u, align_bytes=64) for u in range(2)]
        hid_s = [sb.tile([P, half], U8, name="hid_s%d" % u, align_bytes=64) for u in range(2)]
        tz_g = sb.tile([P, 2, N // P, half], F32, name="tz_g", tag="pw_g3")
        nc.vector.tensor_copy(tz_g[:, 0, 0, :], tz_rows[0][:].indirect(idx7_halves[0]))
        for u in range(2):
            magnitude(u, slice(2, 4))
            nc.vector.quantize_mx(out=hid_w[u][:].bitcast(E5M2), scales=hid_s[u][:], in_=hid[u][:])
        for u, h in ((0, 1), (1, 0), (1, 1)):
            nc.scalar.activation(tz_g[:, u, h, :], tz_rows[h][:].indirect(idx7_halves[u]), ACT.Copy)
        for u in range(2):
            o_cols = slice(u * half, (u + 1) * half)
            p_ps = psum.tile([P, N // P, half], F32, name="p_ps%d" % u, tag="a%d" % u)
            for h in range(N // P):
                nc.tensor.matmul_mx(
                    out=p_ps[:, h, :], lhsT=wb_w[:, 2 * h * P : 2 * (h + 1) * P].bitcast(E2M1),
                    lhsT_scale=wb_s[:, h * P : (h + 1) * P],
                    rhs=hid_w[u][:].bitcast(E5M2), rhs_scale=hid_s[u][:], start=True, stop=True,
                )
            y = sb.tile([P, N // P, half], F32, name="y%d" % u)
            nc.vector.tensor_tensor(y[:], p_ps[:], tz_g[:, u, :, :], ALU.add)
            nc.sync.dma_start(out[:, o_cols].rearrange("(h p) o -> p h o", p=P), y[:])
